import numpy as np
import ml_dtypes


def mxq(x, axis, fmt="e4m3"):
    dtype, down = {"e4m3": (ml_dtypes.float8_e4m3fn, 7), "e5m2": (ml_dtypes.float8_e5m2, 14)}[fmt]
    v = np.moveaxis(np.asarray(x, np.float32).astype(ml_dtypes.bfloat16).astype(np.float64), axis, -1)
    blocks = v.reshape(v.shape[:-1] + (-1, 32))
    amax = np.abs(blocks).max(-1, keepdims=True)
    byte = np.maximum(np.where(amax > 0, np.frexp(amax)[1] - 1 + 127, 0) - down, 1)
    scale = np.exp2(byte - 127.0)
    codes = (blocks / scale).astype(np.float32).astype(dtype).astype(np.float64)
    return np.moveaxis((codes * scale).reshape(v.shape), -1, axis)


WIDE = False


def mx_kscale(k):
    if not WIDE:
        return np.ones(k)
    levels = np.array([10, -10, 5, -5, 0])
    if k % 512:
        return np.exp2(np.random.permutation(np.resize(levels, k // 32))).repeat(32)
    a = np.empty((k // 512, 16))
    for p in range(k // 512):
        a[p, :8] = np.random.permutation(np.resize(levels, 8))
        for g in range(8):
            far = levels[np.abs(levels - a[p, g]) >= 10]
            a[p, g + 8] = far[np.random.randint(len(far))]
    return np.exp2(a.ravel()).repeat(32)


def f64(x):
    return np.asarray(x).astype(np.float64)


def striped(idx):
    return np.tile(idx.reshape(-1, 16).T, (8, 1)).astype(np.uint16)


def unstriped(offs):
    return offs[:16].T.reshape(-1).astype(np.int64)


def pack_weight(w):
    k, n = w.shape
    w = f64(np.asarray(w, np.float32).astype(ml_dtypes.bfloat16)).reshape(k // 32, 32, n)
    amax = np.abs(w).max(1)
    byte = np.clip(np.where(amax > 0, np.frexp(amax)[1] - 1 + 127 - 7, 1), 1, 254)
    scaled = (w * np.exp2(127.0 - byte)[:, None, :]).reshape(k, n).astype(np.float32)
    words = np.ascontiguousarray(scaled.reshape(k // 512, 128, 4, n).transpose(0, 1, 3, 2)).astype(ml_dtypes.float8_e4m3fn).view(np.uint8)
    return words, np.ascontiguousarray(byte.astype(np.uint8).reshape(k // 512, 16, n))


def unpack_weight(words, scales):
    g, p, n, _ = words.shape
    vals = np.ascontiguousarray(words).view(ml_dtypes.float8_e4m3fn).astype(np.float64) * np.repeat(np.exp2(scales.astype(np.float64) - 127.0), 8, axis=1)[..., None]
    return vals.transpose(0, 1, 3, 2).reshape(g * 512, n)


def relu(v):
    return np.maximum(v, 0.0)


K, T, S, D, N, U = 512, 2048, 512, 4, 256, 1024
P = 2 ** 7


def setup_inputs():
    n = np.random.standard_normal
    s = mx_kscale(K)[:, None]
    packed_xT = pack_weight(n((K, T)) * s)
    return {
        "x_words": packed_xT[0],
        "x_scales": packed_xT[1],
        "w1": (n((K, N)) / np.sqrt(K) / s).astype(np.float32),
        "reg": (n((N, U))).astype(np.float32),
        "reach": (np.tile(np.random.uniform(0.2, 1.0, S), (P, 1))).astype(np.float32),
        "offs": striped(np.random.permutation(T)[:S]),
        "info": striped(np.random.permutation(U)[:S]),
    }


def reference(x_words, x_scales, w1, reg, reach, offs, info):
    regg = f64(reg)[:, unstriped(info)]
    xq = unpack_weight(x_words, x_scales)[:, unstriped(offs)]
    y = mxq(f64(w1), 0, "e4m3").T @ xq
    rp = relu(regg) + 0.05
    tot = rp.reshape(len(rp), -1, D).sum(axis=2)
    strat = rp / np.repeat(tot, D, axis=1)
    sy = strat * y
    val = sy.reshape(len(sy), -1, D).sum(axis=2)
    rnew = relu(regg + f64(reach)[:1] * (y - np.repeat(val, D, axis=1)))
    out = f64(reg).copy()
    out[:, unstriped(info)] = rnew
    return out

@@ -1,0 +1,101 @@
+from contextlib import ExitStack
+
+import concourse.mybir as mybir
+
+K, T, S, D, N, U = 512, 2048, 512, 4, 256, 1024
+P = 128
+V = S // D
+FLOPS = 2 * K * N * S
+
+F32 = mybir.dt.float32
+BF16 = mybir.dt.bfloat16
+I32 = mybir.dt.int32
+U32 = mybir.dt.uint32
+U16 = mybir.dt.uint16
+U8 = mybir.dt.uint8
+FP8X4 = mybir.dt.float8_e4m3fn_x4
+ALU = mybir.AluOpType
+ACT = mybir.ActivationFunctionType
+FLOOR = 0.05
+
+
+def tile_picked_ycfr_put_p_kernel(tc, x_words, x_scales, w1, reg, reach, offs, info, out):
+    nc = tc.nc
+    blocks = range(N // P)
+    with ExitStack() as ctx:
+        keep = ctx.enter_context(tc.tile_pool(name="keep", bufs=1))
+        psum = ctx.enter_context(tc.psum_pool(name="psum", bufs=1))
+
+        offs_t = keep.tile([P, S // 16], U16, name="offs_t")
+        info_t = keep.tile([P, S // 16], U16, name="info_t")
+        words = keep.tile([P, T], I32, name="words", align_bytes=64)
+        scales = keep.tile([P, T], U8, name="scales", align_bytes=64)
+        w_raw = keep.tile([P, 4, N], F32, name="w_raw")
+        reach_t = keep.tile([P, S], F32, name="reach_t")
+        regs = [keep.tile([P, U], F32, name=f"reg{b}") for b in blocks]
+
+        nc.vector.memset(scales[:].bitcast(I32), 0)
+        nc.sync.dma_start(info_t[:], info)
+        nc.sync.dma_start(regs[0][:], reg[0:P, :])
+        nc.sync.dma_start(offs_t[:], offs)
+        for q in range(4):
+            nc.scalar.dma_start(scales[32 * q : 32 * q + 4, :].bitcast(I32), x_scales[0, 4 * q : 4 * q + 4, :].bitcast(I32))
+        nc.sync.dma_start(w_raw[:], w1.rearrange("(p j) m -> p j m", j=4))
+        nc.sync.dma_start(words[:], x_words[0].rearrange("p c t -> p (c t)").bitcast(I32))
+        nc.sync.dma_start(regs[1][:], reg[P : 2 * P, :])
+        nc.sync.dma_start(reach_t[:], reach)
+
+        regg = [keep.tile([P, S], F32, name=f"regg{b}") for b in blocks]
+        pos = [keep.tile([P, S], F32, name=f"pos{b}") for b in blocks]
+        tot = [keep.tile([P, V], F32, name=f"tot{b}") for b in blocks]
+        rs = [keep.tile([P, V], F32, name=f"rs{b}") for b in blocks]
+        rtot = [keep.tile([P, V], F32, name=f"rtot{b}") for b in blocks]
+
+        def before_product(b):
+            nc.vector.tensor_copy(regg[b][:], regs[b][:].indirect(info_t[:]))
+            nc.scalar.activation(pos[b][:], regg[b][:], ACT.Relu)
+            nc.vector.tensor_reduce(tot[b][:], pos[b][:].rearrange("p (v d) -> p v d", d=D), mybir.AxisListType.X, ALU.add)
+            nc.scalar.activation(rs[b][:], tot[b][:], ACT.Abs_reciprocal_sqrt, bias=D * FLOOR)
+            nc.scalar.activation(rtot[b][:], rs[b][:], ACT.Square)
+
+        before_product(0)
+        x_sc = keep.tile([P, S], U8, name="x_sc", align_bytes=64)
+        nc.vector.tensor_copy(x_sc[:], scales[:].indirect(offs_t[:]))
+
+        w_bf = keep.tile([P, N, 4], BF16, name="w_bf", align_bytes=64)
+        nc.scalar.copy(w_bf[:].rearrange("p (c i) j -> p c j i", i=4), w_raw[:].rearrange("p j (c i) -> p c j i", i=4))
+        w_codes = keep.tile([P, N], U32, name="w_codes", align_bytes=64)
+        w_sc = keep.tile([P, N], U8, name="w_sc", align_bytes=64)
+        nc.vector.quantize_mx(out=w_codes[:].bitcast(FP8X4), scales=w_sc[:], in_=w_bf[:].rearrange("p m j -> p (m j)"))
+
+        x_codes = keep.tile([P, S], U32, name="x_codes", align_bytes=64)
+        nc.vector.tensor_copy(x_codes[:], words[:].bitcast(U32).indirect(offs_t[:]))
+
+        y = [psum.tile([P, S], F32, name=f"y{b}") for b in blocks]
+        for b in blocks:
+            nc.tensor.matmul_mx(out=y[b][:], lhsT=w_codes[:, b * P : (b + 1) * P].bitcast(FP8X4), lhsT_scale=w_sc[:, b * P : (b + 1) * P],
+                                rhs=x_codes[:].bitcast(FP8X4), rhs_scale=x_sc[:], start=True, stop=True)
+        before_product(1)
+
+        sy = [keep.tile([P, S], F32, name=f"sy{b}") for b in blocks]
+        num = [keep.tile([P, V], F32, name=f"num{b}") for b in blocks]
+        val = [keep.tile([P, V], F32, name=f"val{b}") for b in blocks]
+        dev = [keep.tile([P, S], F32, name=f"dev{b}") for b in blocks]
+        step = [keep.tile([P, S], F32, name=f"step{b}") for b in blocks]
+        kept = [keep.tile([P, S], F32, name=f"kept{b}") for b in blocks]
+        for b in blocks:
+            nc.vector.scalar_tensor_tensor(sy[b][:], pos[b][:], FLOOR, y[b][:], ALU.add, ALU.mult)
+        for b in blocks:
+            nc.vector.tensor_reduce(num[b][:], sy[b][:].rearrange("p (v d) -> p v d", d=D), mybir.AxisListType.X, ALU.add)
+        for b in blocks:
+            nc.vector.tensor_tensor(val[b][:], num[b][:], rtot[b][:], ALU.mult)
+        for b in blocks:
+            nc.vector.tensor_tensor(dev[b][:].rearrange("p (v d) -> p v d", d=D), y[b][:].rearrange("p (v d) -> p v d", d=D),
+                                    val[b][:].unsqueeze(2).to_broadcast([P, V, D]), ALU.subtract)
+        for b in blocks:
+            nc.vector.tensor_tensor(step[b][:], dev[b][:], reach_t[:], ALU.mult)
+        for b in blocks:
+            nc.vector.scalar_tensor_tensor(kept[b][:], regg[b][:], -1.0, step[b][:], ALU.mult, ALU.max)
+        for b in blocks:
+            nc.vector.tensor_tensor(regs[b][:].indirect(info_t[:]), kept[b][:], regg[b][:], ALU.add)
+            nc.sync.dma_start(out[b * P : (b + 1) * P, :], regs[b][:])

@@ -1,10 +1,14 @@
 from contextlib import ExitStack
 
 import concourse.mybir as mybir
+from concourse.masks import make_identity
 
 K, T, S, D, N, U = 512, 2048, 512, 4, 256, 1024
 P = 128
 V = S // D
+PACK = 4
+LIST_ROWS = 16
+FLOOR = 0.05
 FLOPS = 2 * K * N * S
 
 F32 = mybir.dt.float32
@@ -16,86 +20,184 @@ U8 = mybir.dt.uint8
 FP8X4 = mybir.dt.float8_e4m3fn_x4
 ALU = mybir.AluOpType
 ACT = mybir.ActivationFunctionType
-FLOOR = 0.05
+
+ENTRY_HALVES = (slice(0, S // 2), slice(S // 2, S))
+STATE_HALVES = (slice(0, V // 2), slice(V // 2, V))
+SCATTER_CUT = S // 4
+MX_ALIGN = 64
+WORDS_BYTES = 4 * T
+BORDER_COLS = 16
 
 
 def tile_picked_ycfr_put_p_kernel(tc, x_words, x_scales, w1, reg, reach, offs, info, out):
     nc = tc.nc
-    blocks = range(N // P)
+    first, second = slice(0, P), slice(P, 2 * P)
+
+    def by_state(ap):
+        return ap.rearrange("p (v d) -> p v d", d=D)
+
     with ExitStack() as ctx:
         keep = ctx.enter_context(tc.tile_pool(name="keep", bufs=1))
+        scale_space = ctx.enter_context(tc.tile_pool(name="scale_space", bufs=1))
+        table_space = ctx.enter_context(tc.tile_pool(name="table_space", bufs=1))
         psum = ctx.enter_context(tc.psum_pool(name="psum", bufs=1))
 
-        offs_t = keep.tile([P, S // 16], U16, name="offs_t")
-        info_t = keep.tile([P, S // 16], U16, name="info_t")
-        words = keep.tile([P, T], I32, name="words", align_bytes=64)
-        scales = keep.tile([P, T], U8, name="scales", align_bytes=64)
-        w_raw = keep.tile([P, 4, N], F32, name="w_raw")
-        reach_t = keep.tile([P, S], F32, name="reach_t")
-        regs = [keep.tile([P, U], F32, name=f"reg{b}") for b in blocks]
+        offs_t = keep.tile([P, S // LIST_ROWS], U16, name="offs_t")
+        info_t = keep.tile([P, S // LIST_ROWS], U16, name="info_t")
+        scales = scale_space.tile([P, T], U8, name="scales", offset=0, align_bytes=MX_ALIGN)
+        reg0 = keep.tile([P, U], F32, name="reg0")
+        w_raw = keep.tile([P, PACK, N], F32, name="w_raw", tag="w_raw")
+        c_state = keep.tile([P, D], F32, name="c_state")
 
         nc.vector.memset(scales[:].bitcast(I32), 0)
         nc.sync.dma_start(info_t[:], info)
-        nc.sync.dma_start(regs[0][:], reg[0:P, :])
+        nc.sync.dma_start(reg0[:], reg[first, :])
         nc.sync.dma_start(offs_t[:], offs)
         for q in range(4):
-            nc.scalar.dma_start(scales[32 * q : 32 * q + 4, :].bitcast(I32), x_scales[0, 4 * q : 4 * q + 4, :].bitcast(I32))
-        nc.sync.dma_start(w_raw[:], w1.rearrange("(p j) m -> p j m", j=4))
+            nc.sync.dma_start(scales[32 * q : 32 * q + 4, :].bitcast(I32), x_scales[0, 4 * q : 4 * q + 4, :].bitcast(I32))
+        nc.sync.dma_start(w_raw[:], w1.rearrange("(p j) m -> p j m", j=PACK))
+        nc.gpsimd.dma_start(c_state[:], reach[0].rearrange("(v d) -> v d", d=D))
+
+        floor_inv_sq = table_space.tile([P, BORDER_COLS], F32, name="floor_inv_sq", offset=WORDS_BYTES - 2 * BORDER_COLS)
+        floor_sum = keep.tile([P, BORDER_COLS], F32, name="floor_sum")
+        nc.vector.memset(floor_inv_sq[:], float(round((D * FLOOR) ** -2)))
+        nc.scalar.activation(floor_sum[:], floor_inv_sq[:], ACT.Abs_reciprocal_sqrt)
+        words = table_space.tile([P, T], I32, name="words", offset=0)
+        reg1 = table_space.tile([P, U], F32, name="reg1", offset=WORDS_BYTES)
         nc.sync.dma_start(words[:], x_words[0].rearrange("p c t -> p (c t)").bitcast(I32))
-        nc.sync.dma_start(regs[1][:], reg[P : 2 * P, :])
-        nc.sync.dma_start(reach_t[:], reach)
+        nc.sync.dma_start(reg1[:], reg[second, :])
+        ident = keep.tile([P, P], F32, name="ident")
+        make_identity(nc, ident[:])
 
-        regg = [keep.tile([P, S], F32, name=f"regg{b}") for b in blocks]
-        pos = [keep.tile([P, S], F32, name=f"pos{b}") for b in blocks]
-        tot = [keep.tile([P, V], F32, name=f"tot{b}") for b in blocks]
-        rs = [keep.tile([P, V], F32, name=f"rs{b}") for b in blocks]
-        rtot = [keep.tile([P, V], F32, name=f"rtot{b}") for b in blocks]
+        def turn(dst, src, start, stop):
+            nc.tensor.matmul(dst, src, ident[:], start=start, stop=stop, is_transpose=True)
 
-        def before_product(b):
-            nc.vector.tensor_copy(regg[b][:], regs[b][:].indirect(info_t[:]))
-            nc.scalar.activation(pos[b][:], regg[b][:], ACT.Relu)
-            nc.vector.tensor_reduce(tot[b][:], pos[b][:].rearrange("p (v d) -> p v d", d=D), mybir.AxisListType.X, ALU.add)
-            nc.scalar.activation(rs[b][:], tot[b][:], ACT.Abs_reciprocal_sqrt, bias=D * FLOOR)
-            nc.scalar.activation(rtot[b][:], rs[b][:], ACT.Square)
+        def inverse(dst, root, total):
+            nc.scalar.activation(root, total, ACT.Abs_reciprocal_sqrt, bias=floor_sum[:, 0:1])
+            nc.scalar.activation(dst, root, ACT.Square)
 
-        before_product(0)
-        x_sc = keep.tile([P, S], U8, name="x_sc", align_bytes=64)
+        old0 = keep.tile([P, S], F32, name="old0")
+        nc.vector.tensor_copy(old0[:], reg0[:].indirect(info_t[:]))
+        x_sc = keep.tile([P, S], U8, name="x_sc", align_bytes=MX_ALIGN)
         nc.vector.tensor_copy(x_sc[:], scales[:].indirect(offs_t[:]))
 
-        w_bf = keep.tile([P, N, 4], BF16, name="w_bf", align_bytes=64)
+        pos0 = keep.tile([P, S], F32, name="pos0")
+        tot0 = scale_space.tile([P, V], F32, name="tot0", offset=T // 2, align_bytes=MX_ALIGN)
+        nc.scalar.activation(pos0[:], old0[:], ACT.Relu)
+        nc.vector.tensor_reduce(tot0[:], by_state(pos0[:]), mybir.AxisListType.X, ALU.add)
+
+        w_bf = keep.tile([P, N, PACK], BF16, name="w_bf", tag="w_bf", align_bytes=MX_ALIGN)
         nc.scalar.copy(w_bf[:].rearrange("p (c i) j -> p c j i", i=4), w_raw[:].rearrange("p j (c i) -> p c j i", i=4))
-        w_codes = keep.tile([P, N], U32, name="w_codes", align_bytes=64)
-        w_sc = keep.tile([P, N], U8, name="w_sc", align_bytes=64)
+        w_codes = keep.tile([P, N], U32, name="w_codes", align_bytes=MX_ALIGN)
+        w_sc = scale_space.tile([P, N], U8, name="w_sc", offset=0, align_bytes=MX_ALIGN)
         nc.vector.quantize_mx(out=w_codes[:].bitcast(FP8X4), scales=w_sc[:], in_=w_bf[:].rearrange("p m j -> p (m j)"))
+        c_entry = keep.tile([P, S], F32, name="c_entry", tag="w_bf", align_bytes=MX_ALIGN)
+        nc.sync.dma_start(c_entry[:], reach)
+        root0 = keep.tile([P, V], F32, name="root0", tag="w_raw")
+        inv0 = keep.tile([P, V], F32, name="inv0")
+        inverse(inv0[:], root0[:], tot0[:])
 
-        x_codes = keep.tile([P, S], U32, name="x_codes", align_bytes=64)
+        x_codes = keep.tile([P, S], U32, name="x_codes", align_bytes=MX_ALIGN)
         nc.vector.tensor_copy(x_codes[:], words[:].bitcast(U32).indirect(offs_t[:]))
+        old1 = keep.tile([P, S], F32, name="old1")
+        nc.vector.tensor_copy(old1[:], reg1[:].indirect(info_t[:]))
+        base1 = table_space.tile([P, U], F32, name="base1", offset=0)
+        nc.sync.dma_start(base1[:], reg[second, :])
 
-        y = [psum.tile([P, S], F32, name=f"y{b}") for b in blocks]
-        for b in blocks:
-            nc.tensor.matmul_mx(out=y[b][:], lhsT=w_codes[:, b * P : (b + 1) * P].bitcast(FP8X4), lhsT_scale=w_sc[:, b * P : (b + 1) * P],
-                                rhs=x_codes[:].bitcast(FP8X4), rhs_scale=x_sc[:], start=True, stop=True)
-        before_product(1)
+        def product(dst, rows, entries):
+            nc.tensor.matmul_mx(
+                out=dst,
+                lhsT=w_codes[:, rows].bitcast(FP8X4),
+                lhsT_scale=w_sc[:, rows],
+                rhs=x_codes[:, entries].bitcast(FP8X4),
+                rhs_scale=x_sc[:, entries],
+                start=True,
+                stop=True,
+            )
 
-        sy = [keep.tile([P, S], F32, name=f"sy{b}") for b in blocks]
-        num = [keep.tile([P, V], F32, name=f"num{b}") for b in blocks]
-        val = [keep.tile([P, V], F32, name=f"val{b}") for b in blocks]
-        dev = [keep.tile([P, S], F32, name=f"dev{b}") for b in blocks]
-        step = [keep.tile([P, S], F32, name=f"step{b}") for b in blocks]
-        kept = [keep.tile([P, S], F32, name=f"kept{b}") for b in blocks]
-        for b in blocks:
-            nc.vector.scalar_tensor_tensor(sy[b][:], pos[b][:], FLOOR, y[b][:], ALU.add, ALU.mult)
-        for b in blocks:
-            nc.vector.tensor_reduce(num[b][:], sy[b][:].rearrange("p (v d) -> p v d", d=D), mybir.AxisListType.X, ALU.add)
-        for b in blocks:
-            nc.vector.tensor_tensor(val[b][:], num[b][:], rtot[b][:], ALU.mult)
-        for b in blocks:
-            nc.vector.tensor_tensor(dev[b][:].rearrange("p (v d) -> p v d", d=D), y[b][:].rearrange("p (v d) -> p v d", d=D),
-                                    val[b][:].unsqueeze(2).to_broadcast([P, V, D]), ALU.subtract)
-        for b in blocks:
-            nc.vector.tensor_tensor(step[b][:], dev[b][:], reach_t[:], ALU.mult)
-        for b in blocks:
-            nc.vector.scalar_tensor_tensor(kept[b][:], regg[b][:], -1.0, step[b][:], ALU.mult, ALU.max)
-        for b in blocks:
-            nc.vector.tensor_tensor(regs[b][:].indirect(info_t[:]), kept[b][:], regg[b][:], ALU.add)
-            nc.sync.dma_start(out[b * P : (b + 1) * P, :], regs[b][:])
+        y0 = [psum.tile([P, S // 2], F32, name=f"y0_{i}") for i in range(2)]
+        y1 = psum.tile([P, S], F32, name="y1")
+        for bank, h in zip(y0, ENTRY_HALVES):
+            product(bank[:], first, h)
+        product(y1[:], second, slice(0, S))
+
+        pos1 = keep.tile([P, D, V], F32, name="pos1")
+        nc.scalar.activation(pos1[:].rearrange("p d v -> p v d"), by_state(old1[:]), ACT.Relu)
+        y1_dealt = keep.tile([P, D, V], F32, name="y1_dealt")
+        nc.scalar.copy(y1_dealt[:], y1[:].rearrange("p (v d) -> p d v", d=D))
+
+        terms0 = table_space.tile([P, S], F32, name="terms0", offset=WORDS_BYTES)
+        num0 = keep.tile([P, V], F32, name="num0", tag="num0")
+        mix0 = keep.tile([P, V], F32, name="mix0")
+        dev0 = keep.tile([P, S], F32, name="dev0")
+        for bank, h in zip(y0, ENTRY_HALVES):
+            nc.vector.scalar_tensor_tensor(terms0[:, h], pos0[:, h], FLOOR, bank[:], ALU.add, ALU.mult)
+        for h, g in zip(ENTRY_HALVES, STATE_HALVES):
+            nc.vector.tensor_reduce(num0[:, g], by_state(terms0[:, h]), mybir.AxisListType.X, ALU.add)
+        for g in STATE_HALVES:
+            nc.vector.tensor_tensor(mix0[:, g], num0[:, g], inv0[:, g], ALU.mult)
+
+        def deviation(i):
+            spread = mix0[:, STATE_HALVES[i]].unsqueeze(2).to_broadcast([P, V // 2, D])
+            nc.vector.tensor_tensor(by_state(dev0[:, ENTRY_HALVES[i]]), by_state(y0[i][:]), spread, ALU.subtract)
+
+        deviation(0)
+
+        terms1 = keep.tile([P, D, V], F32, name="terms1", tag="num0")
+        nc.vector.scalar_tensor_tensor(terms1[:], pos1[:], FLOOR, y1_dealt[:], ALU.add, ALU.mult)
+        y1_t = psum.tile([P, D, P], F32, name="y1_t")
+        tot1_t = psum.tile([P, P], F32, name="tot1_t")
+        old1_t = psum.tile([P, D, P], F32, name="old1_t")
+        num1_t = psum.tile([P, P], F32, name="num1_t")
+        for d in range(D):
+            turn(tot1_t[:], pos1[:, d, :], d == 0, d == D - 1)
+        root1_t = keep.tile([P, P], F32, name="root1_t")
+        inv1_t = keep.tile([P, P], F32, name="inv1_t")
+        inverse(inv1_t[:], root1_t[:], tot1_t[:])
+        for d in range(D):
+            turn(num1_t[:], terms1[:, d, :], d == 0, d == D - 1)
+        for d in range(D):
+            turn(y1_t[:, d, :], y1_dealt[:, d, :], True, True)
+        for d in range(D):
+            turn(old1_t[:, d, :], by_state(old1[:])[:, :, d], True, True)
+        minus_c_state = keep.tile([P, D], F32, name="minus_c_state")
+        nc.scalar.activation(minus_c_state[:], c_state[:], ACT.Copy, scale=-1.0)
+        gain_t = keep.tile([P, D, P], F32, name="gain_t")
+        old1_t_sbuf = keep.tile([P, D, P], F32, name="old1_t_sbuf")
+        for d in range(D):
+            nc.scalar.activation(gain_t[:, d, :], y1_t[:, d, :], ACT.Copy, scale=c_state[:, d : d + 1])
+        nc.scalar.copy(old1_t_sbuf[:], old1_t[:])
+        sum1 = psum.tile([P, D, V], F32, name="sum1")
+        for d in range(D):
+            turn(sum1[:, d, :], old1_t_sbuf[:, d, :], d == 0, False)
+        for d in range(D):
+            turn(sum1[:, d, :], gain_t[:, d, :], False, False)
+
+        step0 = keep.tile([P, S], F32, name="step0", tag="step0")
+        deviation(1)
+        for h in ENTRY_HALVES:
+            nc.vector.tensor_tensor(step0[:, h], dev0[:, h], c_entry[:, h], ALU.mult)
+        change0 = keep.tile([P, S], F32, name="change0")
+        for h in ENTRY_HALVES:
+            nc.vector.scalar_tensor_tensor(change0[:, h], old0[:, h], -1.0, step0[:, h], ALU.mult, ALU.max)
+
+        def scatter_first(lo, hi):
+            window = reg0[:].indirect(info_t[:, lo // LIST_ROWS : hi // LIST_ROWS])
+            nc.vector.tensor_tensor(window, change0[:, lo:hi], old0[:, lo:hi], ALU.add)
+
+        scatter_first(0, SCATTER_CUT)
+
+        mix1_t = keep.tile([P, P], F32, name="mix1_t", tag="step0")
+        nc.vector.tensor_tensor(mix1_t[:], num1_t[:], inv1_t[:], ALU.mult)
+        loss_t = keep.tile([P, D, P], F32, name="loss_t")
+        for d in range(D):
+            nc.scalar.activation(loss_t[:, d, :], mix1_t[:], ACT.Copy, scale=minus_c_state[:, d : d + 1])
+        for d in range(D):
+            turn(sum1[:, d, :], loss_t[:, d, :], False, d == D - 1)
+        new1 = keep.tile([P, S], F32, name="new1")
+        nc.scalar.activation(by_state(new1[:]), sum1[:].rearrange("p d v -> p v d"), ACT.Relu)
+
+        scatter_first(SCATTER_CUT, S)
+        nc.sync.dma_start(out[first, :], reg0[:])
+        nc.vector.tensor_copy(base1[:].indirect(info_t[:]), new1[:])
+        nc.sync.dma_start(out[second, :], base1[:])

from contextlib import ExitStack

import concourse.mybir as mybir
from concourse.masks import make_identity

K, T, S, D, N, U = 512, 2048, 512, 4, 256, 1024
P = 128
V = S // D
PACK = 4
LIST_ROWS = 16
FLOOR = 0.05
FLOPS = 2 * K * N * S

F32 = mybir.dt.float32
BF16 = mybir.dt.bfloat16
I32 = mybir.dt.int32
U32 = mybir.dt.uint32
U16 = mybir.dt.uint16
U8 = mybir.dt.uint8
FP8X4 = mybir.dt.float8_e4m3fn_x4
ALU = mybir.AluOpType
ACT = mybir.ActivationFunctionType

ENTRY_HALVES = (slice(0, S // 2), slice(S // 2, S))
STATE_HALVES = (slice(0, V // 2), slice(V // 2, V))
SCATTER_CUT = S // 4
MX_ALIGN = 64
WORDS_BYTES = 4 * T
BORDER_COLS = 16


def tile_picked_ycfr_put_p_kernel(tc, x_words, x_scales, w1, reg, reach, offs, info, out):
    nc = tc.nc
    first, second = slice(0, P), slice(P, 2 * P)

    def by_state(ap):
        return ap.rearrange("p (v d) -> p v d", d=D)

    with ExitStack() as ctx:
        keep = ctx.enter_context(tc.tile_pool(name="keep", bufs=1))
        scale_space = ctx.enter_context(tc.tile_pool(name="scale_space", bufs=1))
        table_space = ctx.enter_context(tc.tile_pool(name="table_space", bufs=1))
        psum = ctx.enter_context(tc.psum_pool(name="psum", bufs=1))

        offs_t = keep.tile([P, S // LIST_ROWS], U16, name="offs_t")
        info_t = keep.tile([P, S // LIST_ROWS], U16, name="info_t")
        scales = scale_space.tile([P, T], U8, name="scales", offset=0, align_bytes=MX_ALIGN)
        reg0 = keep.tile([P, U], F32, name="reg0")
        w_raw = keep.tile([P, PACK, N], F32, name="w_raw", tag="w_raw")
        c_state = keep.tile([P, D], F32, name="c_state")

        nc.vector.memset(scales[:].bitcast(I32), 0)
        nc.sync.dma_start(info_t[:], info)
        nc.sync.dma_start(reg0[:], reg[first, :])
        nc.sync.dma_start(offs_t[:], offs)
        for q in range(4):
            nc.sync.dma_start(scales[32 * q : 32 * q + 4, :].bitcast(I32), x_scales[0, 4 * q : 4 * q + 4, :].bitcast(I32))
        nc.sync.dma_start(w_raw[:], w1.rearrange("(p j) m -> p j m", j=PACK))
        nc.gpsimd.dma_start(c_state[:], reach[0].rearrange("(v d) -> v d", d=D))

        floor_inv_sq = table_space.tile([P, BORDER_COLS], F32, name="floor_inv_sq", offset=WORDS_BYTES - 2 * BORDER_COLS)
        floor_sum = keep.tile([P, BORDER_COLS], F32, name="floor_sum")
        nc.vector.memset(floor_inv_sq[:], float(round((D * FLOOR) ** -2)))
        nc.scalar.activation(floor_sum[:], floor_inv_sq[:], ACT.Abs_reciprocal_sqrt)
        words = table_space.tile([P, T], I32, name="words", offset=0)
        reg1 = table_space.tile([P, U], F32, name="reg1", offset=WORDS_BYTES)
        nc.sync.dma_start(words[:], x_words[0].rearrange("p c t -> p (c t)").bitcast(I32))
        nc.sync.dma_start(reg1[:], reg[second, :])
        ident = keep.tile([P, P], F32, name="ident")
        make_identity(nc, ident[:])

        def turn(dst, src, start, stop):
            nc.tensor.matmul(dst, src, ident[:], start=start, stop=stop, is_transpose=True)

        def inverse(dst, root, total):
            nc.scalar.activation(root, total, ACT.Abs_reciprocal_sqrt, bias=floor_sum[:, 0:1])
            nc.scalar.activation(dst, root, ACT.Square)

        old0 = keep.tile([P, S], F32, name="old0")
        nc.vector.tensor_copy(old0[:], reg0[:].indirect(info_t[:]))
        x_sc = keep.tile([P, S], U8, name="x_sc", align_bytes=MX_ALIGN)
        nc.vector.tensor_copy(x_sc[:], scales[:].indirect(offs_t[:]))

        pos0 = keep.tile([P, S], F32, name="pos0")
        tot0 = scale_space.tile([P, V], F32, name="tot0", offset=T // 2, align_bytes=MX_ALIGN)
        nc.scalar.activation(pos0[:], old0[:], ACT.Relu)
        nc.vector.tensor_reduce(tot0[:], by_state(pos0[:]), mybir.AxisListType.X, ALU.add)

        w_bf = keep.tile([P, N, PACK], BF16, name="w_bf", tag="w_bf", align_bytes=MX_ALIGN)
        nc.scalar.copy(w_bf[:].rearrange("p (c i) j -> p c j i", i=4), w_raw[:].rearrange("p j (c i) -> p c j i", i=4))
        w_codes = keep.tile([P, N], U32, name="w_codes", align_bytes=MX_ALIGN)
        w_sc = scale_space.tile([P, N], U8, name="w_sc", offset=0, align_bytes=MX_ALIGN)
        nc.vector.quantize_mx(out=w_codes[:].bitcast(FP8X4), scales=w_sc[:], in_=w_bf[:].rearrange("p m j -> p (m j)"))
        c_entry = keep.tile([P, S], F32, name="c_entry", tag="w_bf", align_bytes=MX_ALIGN)
        nc.sync.dma_start(c_entry[:], reach)
        root0 = keep.tile([P, V], F32, name="root0", tag="w_raw")
        inv0 = keep.tile([P, V], F32, name="inv0")
        inverse(inv0[:], root0[:], tot0[:])

        x_codes = keep.tile([P, S], U32, name="x_codes", align_bytes=MX_ALIGN)
        nc.vector.tensor_copy(x_codes[:], words[:].bitcast(U32).indirect(offs_t[:]))
        old1 = keep.tile([P, S], F32, name="old1")
        nc.vector.tensor_copy(old1[:], reg1[:].indirect(info_t[:]))
        base1 = table_space.tile([P, U], F32, name="base1", offset=0)
        nc.sync.dma_start(base1[:], reg[second, :])

        def product(dst, rows, entries):
            nc.tensor.matmul_mx(
                out=dst,
                lhsT=w_codes[:, rows].bitcast(FP8X4),
                lhsT_scale=w_sc[:, rows],
                rhs=x_codes[:, entries].bitcast(FP8X4),
                rhs_scale=x_sc[:, entries],
                start=True,
                stop=True,
            )

        y0 = [psum.tile([P, S // 2], F32, name=f"y0_{i}") for i in range(2)]
        y1 = psum.tile([P, S], F32, name="y1")
        for bank, h in zip(y0, ENTRY_HALVES):
            product(bank[:], first, h)
        product(y1[:], second, slice(0, S))

        pos1 = keep.tile([P, D, V], F32, name="pos1")
        nc.scalar.activation(pos1[:].rearrange("p d v -> p v d"), by_state(old1[:]), ACT.Relu)
        y1_dealt = keep.tile([P, D, V], F32, name="y1_dealt")
        nc.scalar.copy(y1_dealt[:], y1[:].rearrange("p (v d) -> p d v", d=D))

        terms0 = table_space.tile([P, S], F32, name="terms0", offset=WORDS_BYTES)
        num0 = keep.tile([P, V], F32, name="num0", tag="num0")
        mix0 = keep.tile([P, V], F32, name="mix0")
        dev0 = keep.tile([P, S], F32, name="dev0")
        for bank, h in zip(y0, ENTRY_HALVES):
            nc.vector.scalar_tensor_tensor(terms0[:, h], pos0[:, h], FLOOR, bank[:], ALU.add, ALU.mult)
        for h, g in zip(ENTRY_HALVES, STATE_HALVES):
            nc.vector.tensor_reduce(num0[:, g], by_state(terms0[:, h]), mybir.AxisListType.X, ALU.add)
        for g in STATE_HALVES:
            nc.vector.tensor_tensor(mix0[:, g], num0[:, g], inv0[:, g], ALU.mult)

        def deviation(i):
            spread = mix0[:, STATE_HALVES[i]].unsqueeze(2).to_broadcast([P, V // 2, D])
            nc.vector.tensor_tensor(by_state(dev0[:, ENTRY_HALVES[i]]), by_state(y0[i][:]), spread, ALU.subtract)

        deviation(0)

        terms1 = keep.tile([P, D, V], F32, name="terms1", tag="num0")
        nc.vector.scalar_tensor_tensor(terms1[:], pos1[:], FLOOR, y1_dealt[:], ALU.add, ALU.mult)
        y1_t = psum.tile([P, D, P], F32, name="y1_t")
        tot1_t = psum.tile([P, P], F32, name="tot1_t")
        old1_t = psum.tile([P, D, P], F32, name="old1_t")
        num1_t = psum.tile([P, P], F32, name="num1_t")
        for d in range(D):
            turn(tot1_t[:], pos1[:, d, :], d == 0, d == D - 1)
        root1_t = keep.tile([P, P], F32, name="root1_t")
        inv1_t = keep.tile([P, P], F32, name="inv1_t")
        inverse(inv1_t[:], root1_t[:], tot1_t[:])
        for d in range(D):
            turn(num1_t[:], terms1[:, d, :], d == 0, d == D - 1)
        for d in range(D):
            turn(y1_t[:, d, :], y1_dealt[:, d, :], True, True)
        for d in range(D):
            turn(old1_t[:, d, :], by_state(old1[:])[:, :, d], True, True)
        minus_c_state = keep.tile([P, D], F32, name="minus_c_state")
        nc.scalar.activation(minus_c_state[:], c_state[:], ACT.Copy, scale=-1.0)
        gain_t = keep.tile([P, D, P], F32, name="gain_t")
        old1_t_sbuf = keep.tile([P, D, P], F32, name="old1_t_sbuf")
        for d in range(D):
            nc.scalar.activation(gain_t[:, d, :], y1_t[:, d, :], ACT.Copy, scale=c_state[:, d : d + 1])
        nc.scalar.copy(old1_t_sbuf[:], old1_t[:])
        sum1 = psum.tile([P, D, V], F32, name="sum1")
        for d in range(D):
            turn(sum1[:, d, :], old1_t_sbuf[:, d, :], d == 0, False)
        for d in range(D):
            turn(sum1[:, d, :], gain_t[:, d, :], False, False)

        step0 = keep.tile([P, S], F32, name="step0", tag="step0")
        deviation(1)
        for h in ENTRY_HALVES:
            nc.vector.tensor_tensor(step0[:, h], dev0[:, h], c_entry[:, h], ALU.mult)
        change0 = keep.tile([P, S], F32, name="change0")
        for h in ENTRY_HALVES:
            nc.vector.scalar_tensor_tensor(change0[:, h], old0[:, h], -1.0, step0[:, h], ALU.mult, ALU.max)

        def scatter_first(lo, hi):
            window = reg0[:].indirect(info_t[:, lo // LIST_ROWS : hi // LIST_ROWS])
            nc.vector.tensor_tensor(window, change0[:, lo:hi], old0[:, lo:hi], ALU.add)

        scatter_first(0, SCATTER_CUT)

        mix1_t = keep.tile([P, P], F32, name="mix1_t", tag="step0")
        nc.vector.tensor_tensor(mix1_t[:], num1_t[:], inv1_t[:], ALU.mult)
        loss_t = keep.tile([P, D, P], F32, name="loss_t")
        for d in range(D):
            nc.scalar.activation(loss_t[:, d, :], mix1_t[:], ACT.Copy, scale=minus_c_state[:, d : d + 1])
        for d in range(D):
            turn(sum1[:, d, :], loss_t[:, d, :], False, d == D - 1)
        new1 = keep.tile([P, S], F32, name="new1")
        nc.scalar.activation(by_state(new1[:]), sum1[:].rearrange("p d v -> p v d"), ACT.Relu)

        scatter_first(SCATTER_CUT, S)
        nc.sync.dma_start(out[first, :], reg0[:])
        nc.vector.tensor_copy(base1[:].indirect(info_t[:]), new1[:])
        nc.sync.dma_start(out[second, :], base1[:])
